import numpy as np
import ml_dtypes


def mxq(x, axis, fmt="e4m3"):
    dtype, down = {"e4m3": (ml_dtypes.float8_e4m3fn, 7), "e5m2": (ml_dtypes.float8_e5m2, 14)}[fmt]
    v = np.moveaxis(np.asarray(x, np.float32).astype(ml_dtypes.bfloat16).astype(np.float64), axis, -1)
    blocks = v.reshape(v.shape[:-1] + (-1, 32))
    amax = np.abs(blocks).max(-1, keepdims=True)
    byte = np.maximum(np.where(amax > 0, np.frexp(amax)[1] - 1 + 127, 0) - down, 1)
    scale = np.exp2(byte - 127.0)
    codes = (blocks / scale).astype(np.float32).astype(dtype).astype(np.float64)
    return np.moveaxis((codes * scale).reshape(v.shape), -1, axis)


WIDE = False


def mx_kscale(k):
    if not WIDE:
        return np.ones(k)
    levels = np.array([10, -10, 5, -5, 0])
    if k % 512:
        return np.exp2(np.random.permutation(np.resize(levels, k // 32))).repeat(32)
    a = np.empty((k // 512, 16))
    for p in range(k // 512):
        a[p, :8] = np.random.permutation(np.resize(levels, 8))
        for g in range(8):
            far = levels[np.abs(levels - a[p, g]) >= 10]
            a[p, g + 8] = far[np.random.randint(len(far))]
    return np.exp2(a.ravel()).repeat(32)


def f64(x):
    return np.asarray(x).astype(np.float64)


def striped(idx):
    return np.tile(idx.reshape(-1, 16).T, (8, 1)).astype(np.uint16)


def unstriped(offs):
    return offs[:16].T.reshape(-1).astype(np.int64)


E2M1 = np.array([0.0, 0.5, 1.0, 1.5, 2.0, 3.0, 4.0, 6.0, -0.0, -0.5, -1.0, -1.5, -2.0, -3.0, -4.0, -6.0])


def pack_weight(w, fmt):
    k, n = w.shape
    w = f64(np.asarray(w, np.float32).astype(ml_dtypes.bfloat16)).reshape(k // 32, 32, n)
    amax = np.abs(w).max(1)
    if fmt == "e4m3":
        byte = np.frexp(amax)[1] - 1 + 127 - 7
    else:
        mant, ex = np.frexp(amax / 6.0)
        byte = np.where(mant > 0.5, ex, ex - 1) + 127
    byte = np.clip(np.where(amax > 0, byte, 1), 1, 254)
    scaled = (w * np.exp2(127.0 - byte)[:, None, :]).reshape(k, n).astype(np.float32)
    by_word = np.ascontiguousarray(scaled.reshape(k // 512, 128, 4, n).transpose(0, 1, 3, 2))
    if fmt == "e4m3":
        words = by_word.astype(ml_dtypes.float8_e4m3fn).view(np.uint8)
    else:
        c = by_word.astype(ml_dtypes.float4_e2m1fn).view(np.uint8) & 0xF
        words = (c[..., 0::2] | (c[..., 1::2] << 4)).reshape(k // 512, 128, 2 * n)
    return np.ascontiguousarray(words), np.ascontiguousarray(byte.astype(np.uint8).reshape(k // 512, 16, n))


def unpack_weight(words, scales, fmt):
    g, _, n = scales.shape
    words = np.ascontiguousarray(words).reshape(g, 128, n, -1)
    if fmt == "e4m3":
        vals = words.view(ml_dtypes.float8_e4m3fn).astype(np.float64)
    else:
        nib = np.empty((g, 128, n, 4), np.uint8)
        nib[..., 0::2] = words & 0xF
        nib[..., 1::2] = words >> 4
        vals = E2M1[nib]
    vals = vals * np.repeat(np.exp2(scales.astype(np.float64) - 127.0), 8, axis=1)[..., None]
    return vals.transpose(0, 1, 3, 2).reshape(g * 512, n)


def gelu(v):
    return 0.5 * v * (1.0 + np.tanh(np.sqrt(2.0 / np.pi) * (v + 0.044715 * v**3)))


K, T, S, H, T2, P, N = 1024, 4096, 1024, 1024, 2048, 512, 512

def setup_inputs():
    n = np.random.standard_normal
    s = mx_kscale(K)[:, None]
    u = mx_kscale(H)[:, None]
    tab_words, tab_scales = pack_weight(n((K, T)) * s, "e4m3")
    w1_words, w1_scales = pack_weight(n((K, H)) / np.sqrt(K) / s * u.T, "e2m1")
    perm = np.random.permutation(T2)
    return {
        "tab_words": tab_words, "tab_scales": tab_scales,
        "w1_words": w1_words, "w1_scales": w1_scales,
        "b1": (0.6 * n(H) * u[:, 0]).astype(np.float32),
        "near": n((H, S)).astype(np.float32),
        "wgs": np.exp(0.3 * n((128, S))).astype(np.float32),
        "page0": (n((H, T2)) * u).astype(np.float32),
        "drag": np.exp(0.4 * n(H)).astype(np.float32),
        "w2": (n((H, N)) / np.sqrt(H) / u).astype(np.float32),
        "offs": striped(np.random.permutation(T)[:S]),
        "offs2": striped(np.random.permutation(T2)[:S]),
        "offs3": striped(perm[:P]),
        "offs4": striped(perm[P:2 * P]),
    }

def reference(tab_words, tab_scales, w1_words, w1_scales, b1, near, wgs, page0, drag, w2, offs, offs2, offs3, offs4):
    v = unpack_weight(tab_words, tab_scales, "e4m3")[:, unstriped(offs)]
    w1 = unpack_weight(w1_words, w1_scales, "e2m1")
    x = w1.T @ v
    h = np.abs(x + f64(b1)[:, None]) * f64(near)
    page = f64(page0).copy()
    page[:, unstriped(offs2)] = np.tile(f64(wgs), (H // 128, 1)) * h
    a = page[:, unstriped(offs3)]
    b = page[:, unstriped(offs4)]
    page[:, unstriped(offs3)] = a + b
    page[:, unstriped(offs4)] = f64(drag)[:, None] * np.maximum(a, b)
    pq = mxq(page, 0, "e4m3")
    w2q = mxq(f64(w2), 0, "e4m3")
    return np.tanh(w2q.T @ pq)

@@ -1,0 +1,276 @@
+from contextlib import ExitStack
+
+import concourse.mybir as mybir
+
+K, T, S, H, T2, NPAIR, N = 1024, 4096, 1024, 1024, 2048, 512, 512
+FLOPS = 2 * K * H * S + 2 * H * N * T2
+
+F32 = mybir.dt.float32
+BF16 = mybir.dt.bfloat16
+I32 = mybir.dt.int32
+U32 = mybir.dt.uint32
+U16 = mybir.dt.uint16
+U8 = mybir.dt.uint8
+FP8X4 = mybir.dt.float8_e4m3fn_x4
+FP4X4 = mybir.dt.float4_e2m1fn_x4
+ALU = mybir.AluOpType
+ACT = mybir.ActivationFunctionType
+
+P = 128
+PACK = 4
+BANK = 512
+PASSES = 2
+
+
+def tile_list_slipstream_pair_features_kernel(
+    tc, tab_words, tab_scales, w1_words, w1_scales, b1, near, wgs, page0, drag, w2, offs, offs2, offs3, offs4, out
+):
+    nc = tc.nc
+    with ExitStack() as ctx:
+        lists = ctx.enter_context(tc.tile_pool(name="lists", bufs=1))
+        keep = ctx.enter_context(tc.tile_pool(name="keep", bufs=1))
+        ring = ctx.enter_context(tc.tile_pool(name="ring", bufs=1))
+        psum = ctx.enter_context(tc.psum_pool(name="psum", bufs=1))
+
+        pick = lists.tile([P, S // 16], U16, name="pick")
+        place = lists.tile([P, S // 16], U16, name="place")
+        lead = lists.tile([P, NPAIR // 16], U16, name="lead")
+        chase = lists.tile([P, NPAIR // 16], U16, name="chase")
+
+        tab_sc = ring.tile([P, PASSES, T], U8, name="tab_sc", tag="wide8k", bufs=1, align_bytes=64)
+        w1_sc_raw = keep.tile([P, PASSES, H], U8, name="w1_sc_raw", align_bytes=64)
+        nc.vector.memset(tab_sc[:].bitcast(I32), 0)
+        nc.gpsimd.memset(w1_sc_raw[:].bitcast(I32), 0)
+
+        nc.sync.dma_start(out=pick[:], in_=offs)
+        for r in range(4):
+            nc.scalar.dma_start(
+                out=tab_sc[r:P:32, :, :].bitcast(I32),
+                in_=tab_scales[:, r:16:4, :].rearrange("a q t -> q a t").bitcast(I32),
+            )
+        w1_raw = keep.tile([P, PASSES, 2 * H], U8, name="w1_raw", align_bytes=64)
+        nc.sync.dma_start(out=w1_raw[:].bitcast(I32), in_=w1_words.rearrange("a p c -> p a c").bitcast(I32))
+        tab = []
+        for a in range(PASSES):
+            words = ring.tile([P, T], U32, name=f"tab{a}", tag="wide16k", bufs=2, align_bytes=64)
+            nc.sync.dma_start(out=words[:].bitcast(I32), in_=tab_words[a].rearrange("p t i -> p (t i)").bitcast(I32))
+            tab.append(words)
+        for r in range(4):
+            nc.scalar.dma_start(
+                out=w1_sc_raw[r:P:32, :, :].bitcast(I32),
+                in_=w1_scales[:, r:16:4, :].rearrange("a q c -> q a c").bitcast(I32),
+            )
+        bias = keep.tile([P, PASSES, PACK], F32, name="bias")
+        nc.sync.dma_start(out=bias[:], in_=b1.rearrange("(b p t) -> p b t", b=PASSES, t=PACK))
+
+        page_rows = page0.rearrange("(b p t) c -> b t p c", b=PASSES, t=PACK)
+        near_rows = near.rearrange("(b p t) j -> b p t j", b=PASSES, t=PACK)
+        wgs_rows = wgs.rearrange("(q t) j -> q t j", t=PACK)
+        wgs_sb = keep.tile([P, PACK, S], F32, name="wgs_sb")
+
+        def load_wgs(t0, t1):
+            for quad in range(4):
+                nc.sync.dma_start(out=wgs_sb[32 * quad : 32 * quad + 32, t0:t1, :], in_=wgs_rows[:, t0:t1, :])
+
+        pages = {}
+        factor = {}
+
+        def load_page(i):
+            pages[i] = ring.tile([P, T2], F32, name=f"page{i}", tag="page", bufs=6)
+            nc.sync.dma_start(out=pages[i][:], in_=page_rows[i // PACK, i % PACK])
+
+        def load_near(i, count):
+            b, t = divmod(i, PACK)
+            rows = ring.tile([P, count, S], F32, name=f"near{i}", tag="near", bufs=2)
+            nc.sync.dma_start(out=rows[:], in_=near_rows[b, :, t : t + count, :])
+            return rows
+
+        def weigh(i, count, rows):
+            t = i % PACK
+            nc.vector.tensor_tensor(out=rows[:], in0=rows[:], in1=wgs_sb[:, t : t + count, :], op=ALU.mult)
+            for u in range(count):
+                factor[i + u] = rows[:, u, :]
+
+        load_page(0)
+        near0 = load_near(0, 1)
+        load_wgs(0, 1)
+        nc.sync.dma_start(out=place[:], in_=offs2)
+        nc.sync.dma_start(out=lead[:], in_=offs3)
+        nc.sync.dma_start(out=chase[:], in_=offs4)
+        drag_col = keep.tile([P, PASSES, PACK], F32, name="drag_col")
+        nc.sync.dma_start(out=drag_col[:], in_=drag.rearrange("(b p t) -> p b t", b=PASSES, t=PACK))
+
+        w1_dealt = keep.tile([P, PASSES, 2 * H], U8, name="w1_dealt", align_bytes=64)
+        w1_sc = keep.tile([P, PASSES, H], U8, name="w1_sc", align_bytes=64)
+
+        def deal_w1(b):
+            cols = slice(BANK * b, BANK * (b + 1))
+            nc.vector.tensor_copy(
+                out=w1_dealt[:].bitcast(U16)[:, :, cols].rearrange("p a (t q) -> p a t q", t=PACK),
+                in_=w1_raw[:].bitcast(U16)[:, :, cols].rearrange("p a (q t) -> p a t q", t=PACK),
+            )
+            nc.vector.tensor_copy(
+                out=w1_sc[:, :, cols].rearrange("p a (t q) -> p a t q", t=PACK),
+                in_=w1_sc_raw[:, :, cols].rearrange("p a (q t) -> p a t q", t=PACK),
+            )
+
+        v_sc = []
+        for a in range(PASSES):
+            plane = keep.tile([P, S], U8, name=f"v_sc{a}", align_bytes=64)
+            nc.vector.tensor_copy(out=plane[:], in_=tab_sc[:, a, :].indirect(pick[:]))
+            v_sc.append(plane)
+        deal_w1(0)
+        v_words = {}
+        for a in range(PASSES):
+            for half in range(2):
+                v_words[a, half] = keep.tile([P, BANK], U32, name=f"v_words{a}{half}", align_bytes=64)
+                nc.vector.tensor_copy(
+                    out=v_words[a, half][:], in_=tab[a][:].indirect(pick[:, 32 * half : 32 * half + 32])
+                )
+
+        states = {}
+
+        def first_product(i):
+            b, t = divmod(i, PACK)
+            c0 = BANK * b + P * t
+            states[i] = ring.tile([P, S], F32, name=f"state{i}", tag="state", bufs=4)
+            for half in range(2):
+                acc = psum.tile([P, BANK], F32, name=f"x{i}{half}", tag="x", bufs=2)
+                for a in range(PASSES):
+                    nc.tensor.matmul_mx(
+                        out=acc[:],
+                        lhsT=w1_dealt[:, a, 2 * c0 : 2 * (c0 + P)].bitcast(FP4X4),
+                        lhsT_scale=w1_sc[:, a, c0 : c0 + P],
+                        rhs=v_words[a, half][:].bitcast(FP8X4),
+                        rhs_scale=v_sc[a][:, BANK * half : BANK * (half + 1)],
+                        start=(a == 0),
+                        stop=(a == PASSES - 1),
+                    )
+                nc.scalar.activation(
+                    out=states[i][:, BANK * half : BANK * (half + 1)],
+                    in_=acc[:],
+                    func=ACT.Abs,
+                    bias=bias[:, b, t : t + 1],
+                    scale=1.0,
+                )
+
+        def put_states(i, pieces):
+            width = S // pieces
+            for u in range(pieces):
+                cols = slice(width * u, width * (u + 1))
+                nc.vector.tensor_tensor(
+                    out=pages[i][:].indirect(place[:, width // 16 * u : width // 16 * (u + 1)]),
+                    in0=states[i][:, cols],
+                    in1=factor[i][:, cols],
+                    op=ALU.mult,
+                )
+
+        def exchange(group):
+            a_cols, b_cols, top, spread = {}, {}, {}, {}
+            for i in group:
+                spread[i] = ring.tile([P, NPAIR], F32, name=f"spread{i}", tag="spread", bufs=4)
+                nc.scalar.copy(
+                    out=spread[i][:], in_=drag_col[:, i // PACK, i % PACK : i % PACK + 1].to_broadcast([P, NPAIR])
+                )
+            for i in group:
+                a_cols[i] = ring.tile([P, NPAIR], F32, name=f"a{i}", tag="a", bufs=2)
+                b_cols[i] = ring.tile([P, NPAIR], F32, name=f"b{i}", tag="b", bufs=2)
+                nc.vector.tensor_copy(out=a_cols[i][:], in_=pages[i][:].indirect(lead[:]))
+                nc.vector.tensor_copy(out=b_cols[i][:], in_=pages[i][:].indirect(chase[:]))
+            for i in group:
+                top[i] = ring.tile([P, NPAIR], F32, name=f"top{i}", tag="top", bufs=2)
+                nc.vector.tensor_tensor(out=top[i][:], in0=a_cols[i][:], in1=b_cols[i][:], op=ALU.max)
+            for i in group:
+                nc.vector.tensor_tensor(
+                    out=pages[i][:].indirect(lead[:]), in0=a_cols[i][:], in1=b_cols[i][:], op=ALU.add
+                )
+            for i in group:
+                nc.vector.tensor_tensor(
+                    out=pages[i][:].indirect(chase[:]), in0=top[i][:], in1=spread[i][:], op=ALU.mult
+                )
+
+        woven = {}
+        page_codes = keep.tile([P, PASSES, T2], U32, name="page_codes", align_bytes=64)
+        page_sc = keep.tile([P, PASSES, T2], U8, name="page_sc", align_bytes=64)
+        w2_codes = keep.tile([P, PASSES, N], U32, name="w2_codes", align_bytes=64)
+        w2_sc = keep.tile([P, PASSES, N], U8, name="w2_sc", align_bytes=64)
+
+        def weave(i):
+            b, t = divmod(i, PACK)
+            if t == 0:
+                woven[b] = ring.tile([P, T2, PACK], BF16, name=f"woven{b}", tag="wide16k", bufs=2, align_bytes=64)
+            nc.scalar.copy(out=woven[b][:, :, t], in_=pages[i][:])
+
+        def quantize_page(b, c0, c1):
+            nc.vector.quantize_mx(
+                out=page_codes[:, b, c0:c1].bitcast(FP8X4),
+                scales=page_sc[:, b, c0:c1],
+                in_=woven[b][:, c0:c1, :].rearrange("p c t -> p (c t)"),
+            )
+
+        def quantize_w2(b):
+            raw = ring.tile([P, PACK, N], F32, name=f"w2_raw{b}", tag="wide8k", bufs=1, align_bytes=64)
+            nc.sync.dma_start(out=raw[:], in_=w2[BANK * b : BANK * (b + 1), :].rearrange("(p t) n -> p t n", t=PACK))
+            grouped = ring.tile([P, N, PACK], BF16, name=f"w2_grouped{b}", tag="w2_grouped", bufs=1, align_bytes=64)
+            nc.scalar.copy(out=grouped[:], in_=raw[:].rearrange("p t n -> p n t"))
+            nc.vector.quantize_mx(
+                out=w2_codes[:, b, :].bitcast(FP8X4),
+                scales=w2_sc[:, b, :],
+                in_=grouped[:].rearrange("p n t -> p (n t)"),
+            )
+
+        first_product(0)
+        weigh(0, 1, near0)
+        put_states(0, 2)
+        load_wgs(1, PACK)
+        load_page(1)
+        near1 = load_near(1, 1)
+        first_product(1)
+        deal_w1(1)
+        exchange([0])
+        weigh(1, 1, near1)
+        put_states(1, 1)
+        weave(0)
+        exchange([1])
+        weave(1)
+        for i in (2, 4, 6):
+            load_page(i)
+            load_page(i + 1)
+            rows = load_near(i, 2)
+            first_product(i)
+            first_product(i + 1)
+            weigh(i, 2, rows)
+            put_states(i, 1)
+            put_states(i + 1, 1)
+            if i == 4:
+                quantize_page(0, 0, T2 // 2)
+                quantize_page(0, T2 // 2, T2)
+            if i < 6:
+                quantize_w2(i // 2 - 1)
+            exchange([i, i + 1])
+            if i < 6:
+                weave(i)
+                weave(i + 1)
+
+        last = ring.tile([P, 2, T2], BF16, name="last", tag="wide8k", bufs=1, align_bytes=64)
+        nc.scalar.copy(out=last[:, 0, :], in_=pages[6][:])
+        for c in range(T2 // BANK):
+            cols = slice(BANK * c, BANK * (c + 1))
+            nc.vector.tensor_copy(out=last[:, 1, cols], in_=pages[7][:, cols])
+            nc.vector.tensor_copy(out=woven[1][:, cols, 2:4], in_=last[:, :, cols].rearrange("p u c -> p c u"))
+            quantize_page(1, BANK * c, BANK * (c + 1))
+            for n in range(N // P):
+                acc = psum.tile([P, BANK], F32, name=f"y{c}{n}", tag="y", bufs=6)
+                for b in range(PASSES):
+                    nc.tensor.matmul_mx(
+                        out=acc[:],
+                        lhsT=w2_codes[:, b, P * n : P * (n + 1)].bitcast(FP8X4),
+                        lhsT_scale=w2_sc[:, b, P * n : P * (n + 1)],
+                        rhs=page_codes[:, b, cols].bitcast(FP8X4),
+                        rhs_scale=page_sc[:, b, cols],
+                        start=(b == 0),
+                        stop=(b == PASSES - 1),
+                    )
+                result = ring.tile([P, BANK], F32, name=f"result{c}{n}", tag="result", bufs=8)
+                nc.scalar.activation(out=result[:], in_=acc[:], func=ACT.Tanh)
+                nc.sync.dma_start(out=out[P * n : P * (n + 1), cols], in_=result[:])

@@ -39,29 +39,31 @@ def tile_list_slipstream_pair_features_kernel(
 
         tab_sc = ring.tile([P, PASSES, T], U8, name="tab_sc", tag="wide8k", bufs=1, align_bytes=64)
         w1_sc_raw = keep.tile([P, PASSES, H], U8, name="w1_sc_raw", align_bytes=64)
-        nc.vector.memset(tab_sc[:].bitcast(I32), 0)
-        nc.gpsimd.memset(w1_sc_raw[:].bitcast(I32), 0)
+        nc.vector.memset(tab_sc[:, 0, :].bitcast(I32), 0)
+        nc.gpsimd.memset(tab_sc[:, 1, :].bitcast(I32), 0)
+        nc.vector.memset(w1_sc_raw[:].bitcast(I32), 0)
 
         nc.sync.dma_start(out=pick[:], in_=offs)
+        w1_raw = keep.tile([P, PASSES, 2 * H], U8, name="w1_raw", align_bytes=64)
+        nc.sync.dma_start(out=w1_raw[:].bitcast(I32), in_=w1_words.rearrange("a p c -> p a c").bitcast(I32))
         for r in range(4):
-            nc.scalar.dma_start(
+            nc.sync.dma_start(
                 out=tab_sc[r:P:32, :, :].bitcast(I32),
                 in_=tab_scales[:, r:16:4, :].rearrange("a q t -> q a t").bitcast(I32),
             )
-        w1_raw = keep.tile([P, PASSES, 2 * H], U8, name="w1_raw", align_bytes=64)
-        nc.sync.dma_start(out=w1_raw[:].bitcast(I32), in_=w1_words.rearrange("a p c -> p a c").bitcast(I32))
         tab = []
         for a in range(PASSES):
-            words = ring.tile([P, T], U32, name=f"tab{a}", tag="wide16k", bufs=2, align_bytes=64)
+            words = ring.tile([P, T], U32, name=f"tab{a}", tag=("woven0", "pair")[a], bufs=1, align_bytes=64)
             nc.sync.dma_start(out=words[:].bitcast(I32), in_=tab_words[a].rearrange("p t i -> p (t i)").bitcast(I32))
             tab.append(words)
         for r in range(4):
-            nc.scalar.dma_start(
+            nc.sync.dma_start(
                 out=w1_sc_raw[r:P:32, :, :].bitcast(I32),
                 in_=w1_scales[:, r:16:4, :].rearrange("a q c -> q a c").bitcast(I32),
             )
         bias = keep.tile([P, PASSES, PACK], F32, name="bias")
         nc.sync.dma_start(out=bias[:], in_=b1.rearrange("(b p t) -> p b t", b=PASSES, t=PACK))
+        nc.sync.dma_start(out=place[:], in_=offs2)
 
         page_rows = page0.rearrange("(b p t) c -> b t p c", b=PASSES, t=PACK)
         near_rows = near.rearrange("(b p t) j -> b p t j", b=PASSES, t=PACK)
@@ -85,16 +87,20 @@ def tile_list_slipstream_pair_features_kernel(
             nc.sync.dma_start(out=rows[:], in_=near_rows[b, :, t : t + count, :])
             return rows
 
-        def weigh(i, count, rows):
+        def pair_tile(name):
+            return ring.tile([P, 2, S], F32, name=name, tag="pair", bufs=1, align_bytes=64)
+
+        def weigh(engine, i, count, rows, into):
             t = i % PACK
-            nc.vector.tensor_tensor(out=rows[:], in0=rows[:], in1=wgs_sb[:, t : t + count, :], op=ALU.mult)
+            engine.tensor_tensor(
+                out=into[:, i % 2 : i % 2 + count, :], in0=rows[:], in1=wgs_sb[:, t : t + count, :], op=ALU.mult
+            )
             for u in range(count):
-                factor[i + u] = rows[:, u, :]
+                factor[i + u] = into[:, i % 2 + u, :]
 
         load_page(0)
         near0 = load_near(0, 1)
         load_wgs(0, 1)
-        nc.sync.dma_start(out=place[:], in_=offs2)
         nc.sync.dma_start(out=lead[:], in_=offs3)
         nc.sync.dma_start(out=chase[:], in_=offs4)
         drag_col = keep.tile([P, PASSES, PACK], F32, name="drag_col")
@@ -121,11 +127,12 @@ def tile_list_slipstream_pair_features_kernel(
             v_sc.append(plane)
         deal_w1(0)
         v_words = {}
+        picked = ring.tile([P, PASSES, 2, BANK], U32, name="picked", tag="wide8k", bufs=1, align_bytes=64)
         for a in range(PASSES):
             for half in range(2):
-                v_words[a, half] = keep.tile([P, BANK], U32, name=f"v_words{a}{half}", align_bytes=64)
+                v_words[a, half] = picked[:, a, half, :]
                 nc.vector.tensor_copy(
-                    out=v_words[a, half][:], in_=tab[a][:].indirect(pick[:, 32 * half : 32 * half + 32])
+                    out=v_words[a, half], in_=tab[a][:].indirect(pick[:, 32 * half : 32 * half + 32])
                 )
 
         states = {}
@@ -133,7 +140,10 @@ def tile_list_slipstream_pair_features_kernel(
         def first_product(i):
             b, t = divmod(i, PACK)
             c0 = BANK * b + P * t
-            states[i] = ring.tile([P, S], F32, name=f"state{i}", tag="state", bufs=4)
+            if i < 5:
+                states[i] = ring.tile([P, S], F32, name=f"state{i}", tag="state", bufs=3)
+            else:
+                states[i] = ring.tile([P, S], F32, name=f"state{i}", tag=f"late{i}", bufs=1, align_bytes=64)
             for half in range(2):
                 acc = psum.tile([P, BANK], F32, name=f"x{i}{half}", tag="x", bufs=2)
                 for a in range(PASSES):
@@ -141,7 +151,7 @@ def tile_list_slipstream_pair_features_kernel(
                         out=acc[:],
                         lhsT=w1_dealt[:, a, 2 * c0 : 2 * (c0 + P)].bitcast(FP4X4),
                         lhsT_scale=w1_sc[:, a, c0 : c0 + P],
-                        rhs=v_words[a, half][:].bitcast(FP8X4),
+                        rhs=v_words[a, half].bitcast(FP8X4),
                         rhs_scale=v_sc[a][:, BANK * half : BANK * (half + 1)],
                         start=(a == 0),
                         stop=(a == PASSES - 1),
@@ -166,111 +176,134 @@ def tile_list_slipstream_pair_features_kernel(
                 )
 
         def exchange(group):
-            a_cols, b_cols, top, spread = {}, {}, {}, {}
+            fetched = pair_tile(f"fetched{group[0]}")
+            a_cols = {i: fetched[:, i % 2, 0:NPAIR] for i in group}
+            b_cols = {i: fetched[:, i % 2, NPAIR : 2 * NPAIR] for i in group}
+            slowed = {}
             for i in group:
-                spread[i] = ring.tile([P, NPAIR], F32, name=f"spread{i}", tag="spread", bufs=4)
-                nc.scalar.copy(
-                    out=spread[i][:], in_=drag_col[:, i // PACK, i % PACK : i % PACK + 1].to_broadcast([P, NPAIR])
+                nc.vector.tensor_copy(out=a_cols[i], in_=pages[i][:].indirect(lead[:]))
+                nc.vector.tensor_copy(out=b_cols[i], in_=pages[i][:].indirect(chase[:]))
+            for i in group:
+                top = ring.tile([P, NPAIR], F32, name=f"top{i}", tag="top", bufs=2)
+                nc.vector.tensor_tensor(out=top[:], in0=a_cols[i], in1=b_cols[i], op=ALU.max)
+                slowed[i] = ring.tile([P, NPAIR], F32, name=f"slowed{i}", tag="slowed", bufs=2)
+                nc.scalar.activation(
+                    out=slowed[i][:], in_=top[:], func=ACT.Copy, scale=drag_col[:, i // PACK, i % PACK : i % PACK + 1]
                 )
             for i in group:
-                a_cols[i] = ring.tile([P, NPAIR], F32, name=f"a{i}", tag="a", bufs=2)
-                b_cols[i] = ring.tile([P, NPAIR], F32, name=f"b{i}", tag="b", bufs=2)
-                nc.vector.tensor_copy(out=a_cols[i][:], in_=pages[i][:].indirect(lead[:]))
-                nc.vector.tensor_copy(out=b_cols[i][:], in_=pages[i][:].indirect(chase[:]))
+                nc.vector.tensor_tensor(out=pages[i][:].indirect(lead[:]), in0=a_cols[i], in1=b_cols[i], op=ALU.add)
             for i in group:
-                top[i] = ring.tile([P, NPAIR], F32, name=f"top{i}", tag="top", bufs=2)
-                nc.vector.tensor_tensor(out=top[i][:], in0=a_cols[i][:], in1=b_cols[i][:], op=ALU.max)
-            for i in group:
-                nc.vector.tensor_tensor(
-                    out=pages[i][:].indirect(lead[:]), in0=a_cols[i][:], in1=b_cols[i][:], op=ALU.add
-                )
-            for i in group:
-                nc.vector.tensor_tensor(
-                    out=pages[i][:].indirect(chase[:]), in0=top[i][:], in1=spread[i][:], op=ALU.mult
-                )
+                nc.vector.tensor_copy(out=pages[i][:].indirect(chase[:]), in_=slowed[i][:])
 
         woven = {}
-        page_codes = keep.tile([P, PASSES, T2], U32, name="page_codes", align_bytes=64)
+        page_codes = {}
         page_sc = keep.tile([P, PASSES, T2], U8, name="page_sc", align_bytes=64)
-        w2_codes = keep.tile([P, PASSES, N], U32, name="w2_codes", align_bytes=64)
         w2_sc = keep.tile([P, PASSES, N], U8, name="w2_sc", align_bytes=64)
+        w2_grouped = keep.tile([P, PASSES, N, PACK], BF16, name="w2_grouped", align_bytes=64)
 
         def weave(i):
             b, t = divmod(i, PACK)
             if t == 0:
-                woven[b] = ring.tile([P, T2, PACK], BF16, name=f"woven{b}", tag="wide16k", bufs=2, align_bytes=64)
+                woven[b] = ring.tile([P, T2, PACK], BF16, name=f"woven{b}", tag=f"woven{b}", bufs=1, align_bytes=64)
             nc.scalar.copy(out=woven[b][:, :, t], in_=pages[i][:])
+
+        def codes_at(b, c0, c1):
+            half, at = divmod(c0, S)
+            return page_codes[b, half][:, at : at + c1 - c0].bitcast(FP8X4)
 
         def quantize_page(b, c0, c1):
             nc.vector.quantize_mx(
-                out=page_codes[:, b, c0:c1].bitcast(FP8X4),
+                out=codes_at(b, c0, c1),
                 scales=page_sc[:, b, c0:c1],
                 in_=woven[b][:, c0:c1, :].rearrange("p c t -> p (c t)"),
             )
 
-        def quantize_w2(b):
+        def group_w2(b):
             raw = ring.tile([P, PACK, N], F32, name=f"w2_raw{b}", tag="wide8k", bufs=1, align_bytes=64)
             nc.sync.dma_start(out=raw[:], in_=w2[BANK * b : BANK * (b + 1), :].rearrange("(p t) n -> p t n", t=PACK))
-            grouped = ring.tile([P, N, PACK], BF16, name=f"w2_grouped{b}", tag="w2_grouped", bufs=1, align_bytes=64)
-            nc.scalar.copy(out=grouped[:], in_=raw[:].rearrange("p t n -> p n t"))
-            nc.vector.quantize_mx(
-                out=w2_codes[:, b, :].bitcast(FP8X4),
-                scales=w2_sc[:, b, :],
-                in_=grouped[:].rearrange("p n t -> p (n t)"),
-            )
+            nc.scalar.copy(out=w2_grouped[:, b, :, :], in_=raw[:].rearrange("p t n -> p n t"))
 
         first_product(0)
-        weigh(0, 1, near0)
+        weights = pair_tile("factor0")
+        weigh(nc.vector, 0, 1, near0, weights)
         put_states(0, 2)
-        load_wgs(1, PACK)
+        load_wgs(1, 2)
         load_page(1)
         near1 = load_near(1, 1)
+        load_wgs(2, PACK)
         first_product(1)
         deal_w1(1)
-        exchange([0])
-        weigh(1, 1, near1)
+        weigh(nc.vector, 1, 1, near1, weights)
         put_states(1, 1)
-        weave(0)
-        exchange([1])
-        weave(1)
-        for i in (2, 4, 6):
-            load_page(i)
-            load_page(i + 1)
-            rows = load_near(i, 2)
+        for i in range(2, 8):
             first_product(i)
-            first_product(i + 1)
-            weigh(i, 2, rows)
-            put_states(i, 1)
-            put_states(i + 1, 1)
+        for i in (0, 2, 4, 6):
+            if i > 0:
+                put_states(i, 1)
+                put_states(i + 1, 1)
             if i == 4:
-                quantize_page(0, 0, T2 // 2)
-                quantize_page(0, T2 // 2, T2)
+                w2_codes = ring.tile([P, PASSES, N], U32, name="w2_codes", tag="late5", bufs=1, align_bytes=64)
+                nc.vector.quantize_mx(
+                    out=w2_codes[:].rearrange("p b n -> p (b n)").bitcast(FP8X4),
+                    scales=w2_sc[:].rearrange("p b n -> p (b n)"),
+                    in_=w2_grouped[:].rearrange("p b n t -> p (b n t)"),
+                )
+            if i == 6:
+                for half in range(2):
+                    page_codes[0, half] = ring.tile(
+                        [P, S], U32, name=f"codes0{half}", tag=f"late{6 + half}", bufs=1, align_bytes=64
+                    )
+                    quantize_page(0, S * half, S * (half + 1))
             if i < 6:
-                quantize_w2(i // 2 - 1)
+                load_page(i + 2)
+                load_page(i + 3)
+                rows = load_near(i + 2, 2)
+            if i < 4:
+                group_w2(i // 2)
             exchange([i, i + 1])
             if i < 6:
+                weigh(nc.gpsimd, i + 2, 2, rows, pair_tile(f"factor{i + 2}"))
                 weave(i)
                 weave(i + 1)
 
+        for half in range(2):
+            page_codes[1, half] = keep.tile([P, S], U32, name=f"codes1{half}", align_bytes=64)
         last = ring.tile([P, 2, T2], BF16, name="last", tag="wide8k", bufs=1, align_bytes=64)
         nc.scalar.copy(out=last[:, 0, :], in_=pages[6][:])
-        for c in range(T2 // BANK):
-            cols = slice(BANK * c, BANK * (c + 1))
-            nc.vector.tensor_copy(out=last[:, 1, cols], in_=pages[7][:, cols])
-            nc.vector.tensor_copy(out=woven[1][:, cols, 2:4], in_=last[:, :, cols].rearrange("p u c -> p c u"))
-            quantize_page(1, BANK * c, BANK * (c + 1))
-            for n in range(N // P):
-                acc = psum.tile([P, BANK], F32, name=f"y{c}{n}", tag="y", bufs=6)
+        edges = [0, 256, 512, 1024, 1536, 2048]
+        chunks = list(zip(edges[:-1], edges[1:]))
+        out_rows = out.rearrange("(n p) c -> p n c", p=P)
+
+        def round_last(c0, c1):
+            nc.vector.tensor_copy(out=last[:, 1, c0:c1], in_=pages[7][:, c0:c1])
+
+        banks = 0
+        round_last(*chunks[0])
+        for c, (c0, c1) in enumerate(chunks):
+            if c + 1 < len(chunks):
+                round_last(*chunks[c + 1])
+            nc.vector.tensor_copy(out=woven[1][:, c0:c1, 2:4], in_=last[:, :, c0:c1].rearrange("p u c -> p c u"))
+            quantize_page(1, c0, c1)
+            width = c1 - c0
+            side = BANK // width
+            for n0 in range(0, N // P, side):
+                if banks % 8 < 6:
+                    acc = psum.tile([P, side, width], F32, name=f"y{banks}", tag="y", bufs=6)
+                else:
+                    acc = psum.tile([P, side, width], F32, name=f"y{banks}", tag="x", bufs=2)
                 for b in range(PASSES):
-                    nc.tensor.matmul_mx(
-                        out=acc[:],
-                        lhsT=w2_codes[:, b, P * n : P * (n + 1)].bitcast(FP8X4),
-                        lhsT_scale=w2_sc[:, b, P * n : P * (n + 1)],
-                        rhs=page_codes[:, b, cols].bitcast(FP8X4),
-                        rhs_scale=page_sc[:, b, cols],
-                        start=(b == 0),
-                        stop=(b == PASSES - 1),
-                    )
-                result = ring.tile([P, BANK], F32, name=f"result{c}{n}", tag="result", bufs=8)
+                    for u in range(side):
+                        rows_n = slice(P * (n0 + u), P * (n0 + u + 1))
+                        nc.tensor.matmul_mx(
+                            out=acc[:, u, :],
+                            lhsT=w2_codes[:, b, rows_n].bitcast(FP8X4),
+                            lhsT_scale=w2_sc[:, b, rows_n],
+                            rhs=codes_at(b, c0, c1),
+                            rhs_scale=page_sc[:, b, c0:c1],
+                            start=(b == 0 and u == 0),
+                            stop=(b == PASSES - 1 and u == side - 1),
+                        )
+                result = ring.tile([P, side, width], F32, name=f"result{banks}", tag="result", bufs=8)
                 nc.scalar.activation(out=result[:], in_=acc[:], func=ACT.Tanh)
-                nc.sync.dma_start(out=out[P * n : P * (n + 1), cols], in_=result[:])
+                nc.sync.dma_start(out=out_rows[:, n0 : n0 + side, c0:c1], in_=result[:])
+                banks = banks + 1

from contextlib import ExitStack

import concourse.mybir as mybir

K, T, S, H, T2, NPAIR, N = 1024, 4096, 1024, 1024, 2048, 512, 512
FLOPS = 2 * K * H * S + 2 * H * N * T2

F32 = mybir.dt.float32
BF16 = mybir.dt.bfloat16
I32 = mybir.dt.int32
U32 = mybir.dt.uint32
U16 = mybir.dt.uint16
U8 = mybir.dt.uint8
FP8X4 = mybir.dt.float8_e4m3fn_x4
FP4X4 = mybir.dt.float4_e2m1fn_x4
ALU = mybir.AluOpType
ACT = mybir.ActivationFunctionType

P = 128
PACK = 4
BANK = 512
PASSES = 2


def tile_list_slipstream_pair_features_kernel(
    tc, tab_words, tab_scales, w1_words, w1_scales, b1, near, wgs, page0, drag, w2, offs, offs2, offs3, offs4, out
):
    nc = tc.nc
    with ExitStack() as ctx:
        lists = ctx.enter_context(tc.tile_pool(name="lists", bufs=1))
        keep = ctx.enter_context(tc.tile_pool(name="keep", bufs=1))
        ring = ctx.enter_context(tc.tile_pool(name="ring", bufs=1))
        psum = ctx.enter_context(tc.psum_pool(name="psum", bufs=1))

        pick = lists.tile([P, S // 16], U16, name="pick")
        place = lists.tile([P, S // 16], U16, name="place")
        lead = lists.tile([P, NPAIR // 16], U16, name="lead")
        chase = lists.tile([P, NPAIR // 16], U16, name="chase")

        tab_sc = ring.tile([P, PASSES, T], U8, name="tab_sc", tag="wide8k", bufs=1, align_bytes=64)
        w1_sc_raw = keep.tile([P, PASSES, H], U8, name="w1_sc_raw", align_bytes=64)
        nc.vector.memset(tab_sc[:, 0, :].bitcast(I32), 0)
        nc.gpsimd.memset(tab_sc[:, 1, :].bitcast(I32), 0)
        nc.vector.memset(w1_sc_raw[:].bitcast(I32), 0)

        nc.sync.dma_start(out=pick[:], in_=offs)
        w1_raw = keep.tile([P, PASSES, 2 * H], U8, name="w1_raw", align_bytes=64)
        nc.sync.dma_start(out=w1_raw[:].bitcast(I32), in_=w1_words.rearrange("a p c -> p a c").bitcast(I32))
        for r in range(4):
            nc.sync.dma_start(
                out=tab_sc[r:P:32, :, :].bitcast(I32),
                in_=tab_scales[:, r:16:4, :].rearrange("a q t -> q a t").bitcast(I32),
            )
        tab = []
        for a in range(PASSES):
            words = ring.tile([P, T], U32, name=f"tab{a}", tag=("woven0", "pair")[a], bufs=1, align_bytes=64)
            nc.sync.dma_start(out=words[:].bitcast(I32), in_=tab_words[a].rearrange("p t i -> p (t i)").bitcast(I32))
            tab.append(words)
        for r in range(4):
            nc.sync.dma_start(
                out=w1_sc_raw[r:P:32, :, :].bitcast(I32),
                in_=w1_scales[:, r:16:4, :].rearrange("a q c -> q a c").bitcast(I32),
            )
        bias = keep.tile([P, PASSES, PACK], F32, name="bias")
        nc.sync.dma_start(out=bias[:], in_=b1.rearrange("(b p t) -> p b t", b=PASSES, t=PACK))
        nc.sync.dma_start(out=place[:], in_=offs2)

        page_rows = page0.rearrange("(b p t) c -> b t p c", b=PASSES, t=PACK)
        near_rows = near.rearrange("(b p t) j -> b p t j", b=PASSES, t=PACK)
        wgs_rows = wgs.rearrange("(q t) j -> q t j", t=PACK)
        wgs_sb = keep.tile([P, PACK, S], F32, name="wgs_sb")

        def load_wgs(t0, t1):
            for quad in range(4):
                nc.sync.dma_start(out=wgs_sb[32 * quad : 32 * quad + 32, t0:t1, :], in_=wgs_rows[:, t0:t1, :])

        pages = {}
        factor = {}

        def load_page(i):
            pages[i] = ring.tile([P, T2], F32, name=f"page{i}", tag="page", bufs=6)
            nc.sync.dma_start(out=pages[i][:], in_=page_rows[i // PACK, i % PACK])

        def load_near(i, count):
            b, t = divmod(i, PACK)
            rows = ring.tile([P, count, S], F32, name=f"near{i}", tag="near", bufs=2)
            nc.sync.dma_start(out=rows[:], in_=near_rows[b, :, t : t + count, :])
            return rows

        def pair_tile(name):
            return ring.tile([P, 2, S], F32, name=name, tag="pair", bufs=1, align_bytes=64)

        def weigh(engine, i, count, rows, into):
            t = i % PACK
            engine.tensor_tensor(
                out=into[:, i % 2 : i % 2 + count, :], in0=rows[:], in1=wgs_sb[:, t : t + count, :], op=ALU.mult
            )
            for u in range(count):
                factor[i + u] = into[:, i % 2 + u, :]

        load_page(0)
        near0 = load_near(0, 1)
        load_wgs(0, 1)
        nc.sync.dma_start(out=lead[:], in_=offs3)
        nc.sync.dma_start(out=chase[:], in_=offs4)
        drag_col = keep.tile([P, PASSES, PACK], F32, name="drag_col")
        nc.sync.dma_start(out=drag_col[:], in_=drag.rearrange("(b p t) -> p b t", b=PASSES, t=PACK))

        w1_dealt = keep.tile([P, PASSES, 2 * H], U8, name="w1_dealt", align_bytes=64)
        w1_sc = keep.tile([P, PASSES, H], U8, name="w1_sc", align_bytes=64)

        def deal_w1(b):
            cols = slice(BANK * b, BANK * (b + 1))
            nc.vector.tensor_copy(
                out=w1_dealt[:].bitcast(U16)[:, :, cols].rearrange("p a (t q) -> p a t q", t=PACK),
                in_=w1_raw[:].bitcast(U16)[:, :, cols].rearrange("p a (q t) -> p a t q", t=PACK),
            )
            nc.vector.tensor_copy(
                out=w1_sc[:, :, cols].rearrange("p a (t q) -> p a t q", t=PACK),
                in_=w1_sc_raw[:, :, cols].rearrange("p a (q t) -> p a t q", t=PACK),
            )

        v_sc = []
        for a in range(PASSES):
            plane = keep.tile([P, S], U8, name=f"v_sc{a}", align_bytes=64)
            nc.vector.tensor_copy(out=plane[:], in_=tab_sc[:, a, :].indirect(pick[:]))
            v_sc.append(plane)
        deal_w1(0)
        v_words = {}
        picked = ring.tile([P, PASSES, 2, BANK], U32, name="picked", tag="wide8k", bufs=1, align_bytes=64)
        for a in range(PASSES):
            for half in range(2):
                v_words[a, half] = picked[:, a, half, :]
                nc.vector.tensor_copy(
                    out=v_words[a, half], in_=tab[a][:].indirect(pick[:, 32 * half : 32 * half + 32])
                )

        states = {}

        def first_product(i):
            b, t = divmod(i, PACK)
            c0 = BANK * b + P * t
            if i < 5:
                states[i] = ring.tile([P, S], F32, name=f"state{i}", tag="state", bufs=3)
            else:
                states[i] = ring.tile([P, S], F32, name=f"state{i}", tag=f"late{i}", bufs=1, align_bytes=64)
            for half in range(2):
                acc = psum.tile([P, BANK], F32, name=f"x{i}{half}", tag="x", bufs=2)
                for a in range(PASSES):
                    nc.tensor.matmul_mx(
                        out=acc[:],
                        lhsT=w1_dealt[:, a, 2 * c0 : 2 * (c0 + P)].bitcast(FP4X4),
                        lhsT_scale=w1_sc[:, a, c0 : c0 + P],
                        rhs=v_words[a, half].bitcast(FP8X4),
                        rhs_scale=v_sc[a][:, BANK * half : BANK * (half + 1)],
                        start=(a == 0),
                        stop=(a == PASSES - 1),
                    )
                nc.scalar.activation(
                    out=states[i][:, BANK * half : BANK * (half + 1)],
                    in_=acc[:],
                    func=ACT.Abs,
                    bias=bias[:, b, t : t + 1],
                    scale=1.0,
                )

        def put_states(i, pieces):
            width = S // pieces
            for u in range(pieces):
                cols = slice(width * u, width * (u + 1))
                nc.vector.tensor_tensor(
                    out=pages[i][:].indirect(place[:, width // 16 * u : width // 16 * (u + 1)]),
                    in0=states[i][:, cols],
                    in1=factor[i][:, cols],
                    op=ALU.mult,
                )

        def exchange(group):
            fetched = pair_tile(f"fetched{group[0]}")
            a_cols = {i: fetched[:, i % 2, 0:NPAIR] for i in group}
            b_cols = {i: fetched[:, i % 2, NPAIR : 2 * NPAIR] for i in group}
            slowed = {}
            for i in group:
                nc.vector.tensor_copy(out=a_cols[i], in_=pages[i][:].indirect(lead[:]))
                nc.vector.tensor_copy(out=b_cols[i], in_=pages[i][:].indirect(chase[:]))
            for i in group:
                top = ring.tile([P, NPAIR], F32, name=f"top{i}", tag="top", bufs=2)
                nc.vector.tensor_tensor(out=top[:], in0=a_cols[i], in1=b_cols[i], op=ALU.max)
                slowed[i] = ring.tile([P, NPAIR], F32, name=f"slowed{i}", tag="slowed", bufs=2)
                nc.scalar.activation(
                    out=slowed[i][:], in_=top[:], func=ACT.Copy, scale=drag_col[:, i // PACK, i % PACK : i % PACK + 1]
                )
            for i in group:
                nc.vector.tensor_tensor(out=pages[i][:].indirect(lead[:]), in0=a_cols[i], in1=b_cols[i], op=ALU.add)
            for i in group:
                nc.vector.tensor_copy(out=pages[i][:].indirect(chase[:]), in_=slowed[i][:])

        woven = {}
        page_codes = {}
        page_sc = keep.tile([P, PASSES, T2], U8, name="page_sc", align_bytes=64)
        w2_sc = keep.tile([P, PASSES, N], U8, name="w2_sc", align_bytes=64)
        w2_grouped = keep.tile([P, PASSES, N, PACK], BF16, name="w2_grouped", align_bytes=64)

        def weave(i):
            b, t = divmod(i, PACK)
            if t == 0:
                woven[b] = ring.tile([P, T2, PACK], BF16, name=f"woven{b}", tag=f"woven{b}", bufs=1, align_bytes=64)
            nc.scalar.copy(out=woven[b][:, :, t], in_=pages[i][:])

        def codes_at(b, c0, c1):
            half, at = divmod(c0, S)
            return page_codes[b, half][:, at : at + c1 - c0].bitcast(FP8X4)

        def quantize_page(b, c0, c1):
            nc.vector.quantize_mx(
                out=codes_at(b, c0, c1),
                scales=page_sc[:, b, c0:c1],
                in_=woven[b][:, c0:c1, :].rearrange("p c t -> p (c t)"),
            )

        def group_w2(b):
            raw = ring.tile([P, PACK, N], F32, name=f"w2_raw{b}", tag="wide8k", bufs=1, align_bytes=64)
            nc.sync.dma_start(out=raw[:], in_=w2[BANK * b : BANK * (b + 1), :].rearrange("(p t) n -> p t n", t=PACK))
            nc.scalar.copy(out=w2_grouped[:, b, :, :], in_=raw[:].rearrange("p t n -> p n t"))

        first_product(0)
        weights = pair_tile("factor0")
        weigh(nc.vector, 0, 1, near0, weights)
        put_states(0, 2)
        load_wgs(1, 2)
        load_page(1)
        near1 = load_near(1, 1)
        load_wgs(2, PACK)
        first_product(1)
        deal_w1(1)
        weigh(nc.vector, 1, 1, near1, weights)
        put_states(1, 1)
        for i in range(2, 8):
            first_product(i)
        for i in (0, 2, 4, 6):
            if i > 0:
                put_states(i, 1)
                put_states(i + 1, 1)
            if i == 4:
                w2_codes = ring.tile([P, PASSES, N], U32, name="w2_codes", tag="late5", bufs=1, align_bytes=64)
                nc.vector.quantize_mx(
                    out=w2_codes[:].rearrange("p b n -> p (b n)").bitcast(FP8X4),
                    scales=w2_sc[:].rearrange("p b n -> p (b n)"),
                    in_=w2_grouped[:].rearrange("p b n t -> p (b n t)"),
                )
            if i == 6:
                for half in range(2):
                    page_codes[0, half] = ring.tile(
                        [P, S], U32, name=f"codes0{half}", tag=f"late{6 + half}", bufs=1, align_bytes=64
                    )
                    quantize_page(0, S * half, S * (half + 1))
            if i < 6:
                load_page(i + 2)
                load_page(i + 3)
                rows = load_near(i + 2, 2)
            if i < 4:
                group_w2(i // 2)
            exchange([i, i + 1])
            if i < 6:
                weigh(nc.gpsimd, i + 2, 2, rows, pair_tile(f"factor{i + 2}"))
                weave(i)
                weave(i + 1)

        for half in range(2):
            page_codes[1, half] = keep.tile([P, S], U32, name=f"codes1{half}", align_bytes=64)
        last = ring.tile([P, 2, T2], BF16, name="last", tag="wide8k", bufs=1, align_bytes=64)
        nc.scalar.copy(out=last[:, 0, :], in_=pages[6][:])
        edges = [0, 256, 512, 1024, 1536, 2048]
        chunks = list(zip(edges[:-1], edges[1:]))
        out_rows = out.rearrange("(n p) c -> p n c", p=P)

        def round_last(c0, c1):
            nc.vector.tensor_copy(out=last[:, 1, c0:c1], in_=pages[7][:, c0:c1])

        banks = 0
        round_last(*chunks[0])
        for c, (c0, c1) in enumerate(chunks):
            if c + 1 < len(chunks):
                round_last(*chunks[c + 1])
            nc.vector.tensor_copy(out=woven[1][:, c0:c1, 2:4], in_=last[:, :, c0:c1].rearrange("p u c -> p c u"))
            quantize_page(1, c0, c1)
            width = c1 - c0
            side = BANK // width
            for n0 in range(0, N // P, side):
                if banks % 8 < 6:
                    acc = psum.tile([P, side, width], F32, name=f"y{banks}", tag="y", bufs=6)
                else:
                    acc = psum.tile([P, side, width], F32, name=f"y{banks}", tag="x", bufs=2)
                for b in range(PASSES):
                    for u in range(side):
                        rows_n = slice(P * (n0 + u), P * (n0 + u + 1))
                        nc.tensor.matmul_mx(
                            out=acc[:, u, :],
                            lhsT=w2_codes[:, b, rows_n].bitcast(FP8X4),
                            lhsT_scale=w2_sc[:, b, rows_n],
                            rhs=codes_at(b, c0, c1),
                            rhs_scale=page_sc[:, b, c0:c1],
                            start=(b == 0 and u == 0),
                            stop=(b == PASSES - 1 and u == side - 1),
                        )
                result = ring.tile([P, side, width], F32, name=f"result{banks}", tag="result", bufs=8)
                nc.scalar.activation(out=result[:], in_=acc[:], func=ACT.Tanh)
                nc.sync.dma_start(out=out_rows[:, n0 : n0 + side, c0:c1], in_=result[:])
                banks = banks + 1
